import numpy as np
import ml_dtypes


def mxq(x, axis, fmt="e4m3"):
    dtype, down = {"e4m3": (ml_dtypes.float8_e4m3fn, 7), "e5m2": (ml_dtypes.float8_e5m2, 14)}[fmt]
    v = np.moveaxis(np.asarray(x, np.float32).astype(ml_dtypes.bfloat16).astype(np.float64), axis, -1)
    blocks = v.reshape(v.shape[:-1] + (-1, 32))
    amax = np.abs(blocks).max(-1, keepdims=True)
    byte = np.maximum(np.where(amax > 0, np.frexp(amax)[1] - 1 + 127, 0) - down, 1)
    scale = np.exp2(byte - 127.0)
    codes = (blocks / scale).astype(np.float32).astype(dtype).astype(np.float64)
    return np.moveaxis((codes * scale).reshape(v.shape), -1, axis)


WIDE = False


def mx_kscale(k):
    if not WIDE:
        return np.ones(k)
    levels = np.array([10, -10, 5, -5, 0])
    if k % 512:
        return np.exp2(np.random.permutation(np.resize(levels, k // 32))).repeat(32)
    a = np.empty((k // 512, 16))
    for p in range(k // 512):
        a[p, :8] = np.random.permutation(np.resize(levels, 8))
        for g in range(8):
            far = levels[np.abs(levels - a[p, g]) >= 10]
            a[p, g + 8] = far[np.random.randint(len(far))]
    return np.exp2(a.ravel()).repeat(32)


def f64(x):
    return np.asarray(x).astype(np.float64)


def striped(idx):
    return np.tile(np.asarray(idx).reshape(-1, 16).T, (8, 1)).astype(np.uint16)


def unstriped(offs):
    return offs[:16].T.reshape(-1).astype(np.int64)


E2M1 = np.array([0.0, 0.5, 1.0, 1.5, 2.0, 3.0, 4.0, 6.0, -0.0, -0.5, -1.0, -1.5, -2.0, -3.0, -4.0, -6.0])


def pack_weight(w, fmt):
    k, n = w.shape
    w = f64(np.asarray(w, np.float32).astype(ml_dtypes.bfloat16)).reshape(k // 32, 32, n)
    amax = np.abs(w).max(1)
    if fmt == "e4m3":
        byte = np.frexp(amax)[1] - 1 + 127 - 7
    else:
        mant, ex = np.frexp(amax / 6.0)
        byte = np.where(mant > 0.5, ex, ex - 1) + 127
    byte = np.clip(np.where(amax > 0, byte, 1), 1, 254)
    scaled = (w * np.exp2(127.0 - byte)[:, None, :]).reshape(k, n).astype(np.float32)
    by_word = np.ascontiguousarray(scaled.reshape(k // 512, 128, 4, n).transpose(0, 1, 3, 2))
    if fmt == "e4m3":
        words = by_word.astype(ml_dtypes.float8_e4m3fn).view(np.uint8)
    else:
        c = by_word.astype(ml_dtypes.float4_e2m1fn).view(np.uint8) & 0xF
        words = (c[..., 0::2] | (c[..., 1::2] << 4)).reshape(k // 512, 128, 2 * n)
    return np.ascontiguousarray(words), np.ascontiguousarray(byte.astype(np.uint8).reshape(k // 512, 16, n))


def unpack_weight(words, scales, fmt):
    g, _, n = scales.shape
    words = np.ascontiguousarray(words).reshape(g, 128, n, -1)
    if fmt == "e4m3":
        vals = words.view(ml_dtypes.float8_e4m3fn).astype(np.float64)
    else:
        nib = np.empty((g, 128, n, 4), np.uint8)
        nib[..., 0::2] = words & 0xF
        nib[..., 1::2] = words >> 4
        vals = E2M1[nib]
    vals = vals * np.repeat(np.exp2(scales.astype(np.float64) - 127.0), 8, axis=1)[..., None]
    return vals.transpose(0, 1, 3, 2).reshape(g * 512, n)


def bf(x):
    return np.asarray(x, np.float32).astype(ml_dtypes.bfloat16)


def planes(Y):
    r, m = Y.shape
    b = f64(bf(Y)).reshape(r // 32, 32, m)
    amax = np.abs(b).max(1)
    byte = np.clip(np.where(amax > 0, np.frexp(amax)[1] - 1 + 127 - 7, 1), 1, 254)
    codes = (b * np.exp2(127.0 - byte)[:, None, :]).reshape(r, m).astype(np.float32).astype(ml_dtypes.float8_e4m3fn).view(np.uint8)
    words = codes.reshape(r // 512, 128, 4, m).transpose(0, 1, 3, 2)
    return np.ascontiguousarray(words), np.ascontiguousarray(byte.astype(np.uint8).reshape(r // 512, 16, m))


K, T, J, B, R, N = 512, 2048, 512, 128, 512, 512


def setup_inputs():
    n = np.random.standard_normal
    idx = np.random.permutation(T)[:J]
    fk = mx_kscale(K)
    fr = mx_kscale(R)
    xtp = pack_weight(n((K, T)) / fk[:, None], "e2m1")
    wap = pack_weight(n((K, R)) * 1 / np.sqrt(K) * fk[:, None] * fr, "e4m3")
    wbp = pack_weight(n((R, N)) * 1 / np.sqrt(R) / fr[:, None], "e2m1")
    return {
        "xt_words": xtp[0],
        "xt_scales": xtp[1],
        "wa_words": wap[0],
        "wa_scales": wap[1],
        "wb_words": wbp[0],
        "wb_scales": wbp[1],
        "rw": (np.random.uniform(0.5, 2.0, (1, J))).astype(np.float32),
        "offs": striped(idx),
    }


def reference(xt_words, xt_scales, wa_words, wa_scales, wb_words, wb_scales, rw, offs):
    idx = unstriped(offs)
    xtu = unpack_weight(xt_words, xt_scales, "e2m1")
    wau = unpack_weight(wa_words, wa_scales, "e4m3")
    wbu = unpack_weight(wb_words, wb_scales, "e2m1")
    xtidxg = xtu[:, idx]
    a = wau.T @ xtidxg
    m1 = a.reshape(R, B, J // B).mean(axis=2)
    mr1 = np.repeat(m1, J // B, axis=1)
    hid = a - mr1
    hidq = mxq(hid, 0, "e4m3")
    p = wbu.T @ hidq
    y = p * f64(rw)
    words, scales = planes(y)
    return y, words, scales

from contextlib import ExitStack

import concourse.mybir as mybir
from concourse.masks import make_identity

K, T, J, R, N = 512, 2048, 512, 512, 512
FLOPS = 2 * K * R * J + 2 * R * N * J

F32 = mybir.dt.float32
BF16 = mybir.dt.bfloat16
I32 = mybir.dt.int32
U32 = mybir.dt.uint32
U16 = mybir.dt.uint16
U8 = mybir.dt.uint8
FP8X4 = mybir.dt.float8_e4m3fn_x4
FP4X4 = mybir.dt.float4_e2m1fn_x4
ALU = mybir.AluOpType

P = 128
PACK = 4
GROUP = 4
CHUNK = 128
CHUNKS = J // CHUNK
GROUPS = CHUNK // GROUP


def load_scale_rows(queue, plane, rows):
    for r in range(4):
        queue.dma_start(out=plane[r:P:32, :].bitcast(I32), in_=rows[r:16:4, :].bitcast(I32))


def deal(nc, dst, src, run):
    nc.vector.tensor_copy(
        out=dst.rearrange("p (t g i) -> p g t i", t=PACK, i=run),
        in_=src.rearrange("p (g i t) -> p g t i", t=PACK, i=run),
    )


def tile_list_hidden_relative_to_group_pl_kernel(
    tc, xt_words, xt_scales, wa_words, wa_scales, wb_words, wb_scales, rw, offs, out_0, out_1, out_2
):
    nc = tc.nc
    with ExitStack() as ctx:
        keep = ctx.enter_context(tc.tile_pool(name="keep", bufs=1))
        psum = ctx.enter_context(tc.psum_pool(name="psum", bufs=1))

        offsets = keep.tile([P, J // 16], U16, name="offsets")
        xw_all = keep.tile([P, T], U16, name="xw_all", align_bytes=64)
        xs_all = keep.tile([P, T], U8, name="xs_all", align_bytes=64)
        xw = keep.tile([P, J], U16, name="xw", align_bytes=64)
        xs = keep.tile([P, J], U8, name="xs", align_bytes=64)
        waw_raw = keep.tile([P, R], I32, name="waw_raw", align_bytes=64)
        was_raw = keep.tile([P, R], U8, name="was_raw", align_bytes=64)
        wbw_raw = keep.tile([P, N], U16, name="wbw_raw", align_bytes=64)
        wbs_raw = keep.tile([P, N], U8, name="wbs_raw", align_bytes=64)
        waw = keep.tile([P, R], I32, name="waw", align_bytes=64)
        was = keep.tile([P, R], U8, name="was", align_bytes=64)
        wbw = keep.tile([P, N], U16, name="wbw", align_bytes=64)
        wbs = keep.tile([P, N], U8, name="wbs", align_bytes=64)
        rw_col = keep.tile([P, 4], F32, name="rw_col")
        rw_row = keep.tile([P, J], F32, name="rw_row")
        ident = keep.tile([P, P], F32, name="ident")
        hid_codes = keep.tile([P, J], U32, name="hid_codes", align_bytes=64)
        hid_scales = keep.tile([P, J], U8, name="hid_scales", align_bytes=64)
        y_codes = keep.tile([P, J], U32, name="y_codes", align_bytes=64)
        y_scales = keep.tile([P, J], U8, name="y_scales", align_bytes=64)

        nc.vector.memset(xs_all[:].bitcast(I32), 0)
        nc.vector.memset(was_raw[:].bitcast(I32), 0)
        nc.vector.memset(wbs_raw[:].bitcast(I32), 0)

        nc.sync.dma_start(offsets[:], offs)
        load_scale_rows(nc.scalar, xs_all, xt_scales[0])
        nc.sync.dma_start(out=xw_all[:].bitcast(I32), in_=xt_words[0].bitcast(I32))
        nc.sync.dma_start(out=waw_raw[:], in_=wa_words[0].rearrange("p n t -> p (n t)").bitcast(I32))
        nc.gpsimd.dma_start(out=rw_col[:], in_=rw[0].rearrange("(p c) -> p c", c=4))
        load_scale_rows(nc.sync, was_raw, wa_scales[0])
        nc.sync.dma_start(out=wbw_raw[:].bitcast(I32), in_=wb_words[0].bitcast(I32))
        load_scale_rows(nc.sync, wbs_raw, wb_scales[0])

        make_identity(nc, ident[:])
        rw_bank = psum.tile([P, 4, P], F32, name="rw_bank", tag="p3")
        for c in range(4):
            nc.tensor.transpose(rw_bank[:, c, :], rw_col[:, c : c + 1].to_broadcast([P, P]), ident[:])
        nc.scalar.copy(
            out=rw_row[:].rearrange("q (p c) -> q p c", c=4), in_=rw_bank[:].rearrange("q c p -> q p c")
        )

        nc.vector.tensor_copy(xs[:], xs_all[:].indirect(offsets[:]))
        nc.vector.tensor_copy(xw[:], xw_all[:].indirect(offsets[:]))
        deal(nc, waw[:], waw_raw[:], 4)
        deal(nc, was[:], was_raw[:], 16)

        a_bank = [psum.tile([P, PACK, CHUNK], F32, name=f"a{c}", tag=f"a{c}") for c in range(CHUNKS)]
        upper = [keep.tile([P, PACK * GROUPS, 2], F32, name=f"upper{c}") for c in range(CHUNKS)]
        pairs = [keep.tile([P, PACK * GROUPS, 2], F32, name=f"pairs{c}") for c in range(CHUNKS)]
        mean = [keep.tile([P, GROUPS, PACK], F32, name=f"mean{c}") for c in range(CHUNKS)]
        hid = [keep.tile([P, CHUNK, PACK], BF16, name=f"hid{c}", align_bytes=64) for c in range(CHUNKS)]
        y = [keep.tile([P, PACK, CHUNK], F32, name=f"y{c}") for c in range(CHUNKS)]
        y16 = [keep.tile([P, CHUNK, PACK], BF16, name=f"y16_{c}", align_bytes=64) for c in range(CHUNKS)]
        p_bank = {}
        y_rows = out_0.rearrange("(p t) j -> p t j", t=PACK)
        code_rows = out_1[0].rearrange("p n t -> p (n t)").bitcast(I32)

        def cols(c):
            return slice(c * CHUNK, (c + 1) * CHUNK)

        def first_layer(c):
            for t in range(PACK):
                nc.tensor.matmul_mx(
                    out=a_bank[c][:, t, :],
                    lhsT=waw[:, cols(t)].bitcast(FP8X4),
                    lhsT_scale=was[:, cols(t)],
                    rhs=xw[:, cols(c)].bitcast(FP4X4),
                    rhs_scale=xs[:, cols(c)],
                    start=True,
                    stop=True,
                )
            slots = a_bank[c][:].rearrange("p t (b i) -> p (t b) i", i=GROUP)
            nc.scalar.mul(upper[c][:], slots[:, :, 2:4], 1.0 / GROUP)

        def pair_sums(c):
            slots = a_bank[c][:].rearrange("p t (b i) -> p (t b) i", i=GROUP)
            nc.vector.scalar_tensor_tensor(
                out=pairs[c][:], in0=slots[:, :, 0:2], scalar=1.0 / GROUP, in1=upper[c][:],
                op0=ALU.mult, op1=ALU.add,
            )

        def group_mean(c):
            halves = pairs[c][:].rearrange("p (t b) h -> p b t h", t=PACK)
            nc.vector.tensor_tensor(mean[c][:], halves[:, :, :, 0], halves[:, :, :, 1], ALU.add)

        def centre(c):
            nc.vector.tensor_tensor(
                hid[c][:].rearrange("p (b i) t -> p b i t", i=GROUP),
                a_bank[c][:].rearrange("p t (b i) -> p b i t", i=GROUP),
                mean[c][:].unsqueeze(2).to_broadcast([P, GROUPS, GROUP, PACK]),
                ALU.subtract,
            )

        def second_layer(c):
            nc.vector.quantize_mx(
                out=hid_codes[:, cols(c)].bitcast(FP8X4),
                scales=hid_scales[:, cols(c)],
                in_=hid[c][:].rearrange("p j t -> p (j t)"),
            )
            p_bank[c] = psum.tile([P, PACK, CHUNK], F32, name=f"p{c}", tag=f"p{c}")
            for t in range(PACK):
                nc.tensor.matmul_mx(
                    out=p_bank[c][:, t, :],
                    lhsT=wbw[:, cols(t)].bitcast(FP4X4),
                    lhsT_scale=wbs[:, cols(t)],
                    rhs=hid_codes[:, cols(c)].bitcast(FP8X4),
                    rhs_scale=hid_scales[:, cols(c)],
                    start=True,
                    stop=True,
                )

        def weigh(c):
            nc.vector.tensor_tensor(
                y[c][:],
                p_bank[c][:],
                rw_row[:, cols(c)].unsqueeze(1).to_broadcast([P, PACK, CHUNK]),
                ALU.mult,
            )
            nc.sync.dma_start(out=y_rows[:, :, cols(c)], in_=y[c][:])
            nc.scalar.copy(
                out=y16[c][:].rearrange("p (g i) t -> p g t i", i=4),
                in_=y[c][:].rearrange("p t (g i) -> p g t i", i=4),
            )

        def planes(c):
            nc.vector.quantize_mx(
                out=y_codes[:, cols(c)].bitcast(FP8X4),
                scales=y_scales[:, cols(c)],
                in_=y16[c][:].rearrange("p j t -> p (j t)"),
            )

        for c in range(CHUNKS):
            first_layer(c)
        deal(nc, wbw[:], wbw_raw[:], 8)
        pair_sums(0)
        pair_sums(1)
        group_mean(0)
        deal(nc, wbs[:], wbs_raw[:], 16)
        centre(0)
        group_mean(1)
        pair_sums(2)
        second_layer(0)
        centre(1)
        group_mean(2)
        pair_sums(3)
        second_layer(1)
        centre(2)
        group_mean(3)
        weigh(0)
        second_layer(2)
        centre(3)
        weigh(1)
        second_layer(3)
        planes(0)
        weigh(2)
        planes(1)
        weigh(3)
        planes(2)
        nc.sync.dma_start(out=code_rows[:, 0 : 3 * CHUNK], in_=y_codes[:, 0 : 3 * CHUNK].bitcast(I32))
        planes(3)
        nc.sync.dma_start(out=code_rows[:, cols(3)], in_=y_codes[:, cols(3)].bitcast(I32))
        for r in range(4):
            queue = nc.scalar if r % 2 == 0 else nc.sync
            queue.dma_start(out=out_2[0][r:16:4, :].bitcast(I32), in_=y_scales[r:P:32, :].bitcast(I32))
